import numpy as np
import ml_dtypes


def mxq(x, axis, fmt="e4m3"):
    dtype, down = {"e4m3": (ml_dtypes.float8_e4m3fn, 7), "e5m2": (ml_dtypes.float8_e5m2, 14)}[fmt]
    v = np.moveaxis(np.asarray(x, np.float32).astype(ml_dtypes.bfloat16).astype(np.float64), axis, -1)
    blocks = v.reshape(v.shape[:-1] + (-1, 32))
    amax = np.abs(blocks).max(-1, keepdims=True)
    byte = np.maximum(np.where(amax > 0, np.frexp(amax)[1] - 1 + 127, 0) - down, 1)
    scale = np.exp2(byte - 127.0)
    codes = (blocks / scale).astype(np.float32).astype(dtype).astype(np.float64)
    return np.moveaxis((codes * scale).reshape(v.shape), -1, axis)


WIDE = False


def mx_kscale(k, group=512):
    if not WIDE:
        return np.ones(k)
    levels = np.array([18, -18])
    if group != 512:
        return np.exp2(np.random.permutation(np.resize(levels, k // group))).repeat(group)
    if k % 512:
        return np.exp2(np.random.permutation(np.resize(levels, k // 32))).repeat(32)
    a = np.empty((k // 512, 16))
    for p in range(k // 512):
        a[p, :8] = np.random.permutation(np.resize(levels, 8))
        for g in range(8):
            far = levels[np.abs(levels - a[p, g]) >= 10]
            a[p, g + 8] = far[np.random.randint(len(far))]
    return np.exp2(a.ravel()).repeat(32)


def f64(x):
    return np.asarray(x).astype(np.float64)


G, D, M, O, N = 4, 128, 128, 128, 512


def sgn(shape):
    return np.random.uniform(0.5, 2.0, shape) * np.where(np.random.standard_normal(shape) < 0, -1.0, 1.0)


def setup_inputs():
    n = np.random.standard_normal
    s_d = mx_kscale(D, 0)
    s_m = mx_kscale(M, 0)
    return {
        "x": (n((G, D, N)) * s_d[:, None]).astype(np.float32),
        "w1": (n((G, D, M)) / np.sqrt(D) / s_d[:, None]).astype(np.float32),
        "w2": (n((G, D, M)) / np.sqrt(D) / s_d[:, None]).astype(np.float32),
        "fl": (np.random.uniform(0.05, 0.3, (G, M, 1))).astype(np.float32),
        "hs": (sgn((G, M, 1)) * s_m[:, None]).astype(np.float32),
        "wo2": (n((G, M, O)) / np.sqrt(M) / s_m[:, None]).astype(np.float32),
        "res": (0.5 * n((G, O, N))).astype(np.float32),
    }


def reference(x, w1, w2, fl, hs, wo2, res):
    w1q = mxq(f64(w1), 1, "e4m3")
    xq = mxq(f64(x), 1, "e4m3")
    z1 = w1q.transpose(0, 2, 1) @ xq
    w2q = mxq(f64(w2), 1, "e4m3")
    z2 = w2q.transpose(0, 2, 1) @ xq
    e1 = np.exp(np.square(z1) * (-1.0))
    e2 = np.exp(np.square(z2) * (-1.0))
    h = e1 / (e1 + e2 + f64(fl)) * z2
    hh = h * f64(hs)
    wo2q = mxq(f64(wo2), 1, "e4m3")
    hhq = mxq(hh, 1, "e4m3")
    y0 = wo2q.transpose(0, 2, 1) @ hhq
    y = y0 + f64(res)
    return y

@@ -1,0 +1,190 @@
+from contextlib import ExitStack
+
+import concourse.mybir as mybir
+
+G, D, M, O, N = 4, 128, 128, 128, 512
+FLOPS = 2 * G * N * (2 * D * M + M * O)
+
+F32 = mybir.dt.float32
+BF16 = mybir.dt.bfloat16
+U32 = mybir.dt.uint32
+U8 = mybir.dt.uint8
+FP8X4 = mybir.dt.float8_e4m3fn_x4
+ACT = mybir.ActivationFunctionType
+ALU = mybir.AluOpType
+
+P = 128
+PACK = 4
+ROWS = 32
+NMM = 128
+X_CHUNKS = ((0, 128), (128, 256), (256, 512))
+H_CHUNKS = ((0, 128), (128, 256), (256, 384), (384, 512))
+
+
+def interleave_views(grouped, raw):
+    return (
+        grouped.rearrange("p (c i) j -> p c j i", i=4),
+        raw.rearrange("p j (c i) -> p c j i", i=4),
+    )
+
+
+def quantize(nc, codes, scales, grouped):
+    nc.vector.quantize_mx(
+        out=codes.bitcast(FP8X4), scales=scales, in_=grouped.rearrange("p w j -> p (w j)")
+    )
+
+
+def grouped_product(nc, banks, w_codes, w_scales, codes, scales, n0, n1, off):
+    for c0 in range(n0, n1, NMM):
+        for g in range(G):
+            rows = slice(ROWS * g, ROWS * (g + 1))
+            cols = slice(c0 - off, c0 - off + NMM)
+            nc.tensor.matmul_mx(
+                out=banks[g][:, c0 : c0 + NMM],
+                lhsT=w_codes[rows, :].bitcast(FP8X4),
+                lhsT_scale=w_scales[rows, :],
+                rhs=codes[rows, cols].bitcast(FP8X4),
+                rhs_scale=scales[rows, cols],
+                start=True,
+                stop=True,
+            )
+
+
+def tile_rows_fgaussshare_kernel(tc, x, w1, w2, fl, hs, wo2, res, out):
+    nc = tc.nc
+    with ExitStack() as ctx:
+        sb = ctx.enter_context(tc.tile_pool(name="sb", bufs=1))
+        ps = ctx.enter_context(tc.psum_pool(name="ps", bufs=1))
+        ctx.enter_context(tc.manual_schedule())
+
+        bank_a = [ps.tile([P, N], F32, name="bank_a%d" % g) for g in range(G)]
+        bank_b = [ps.tile([P, N], F32, name="bank_b%d" % g) for g in range(G)]
+
+        def packed_view(t):
+            return t.rearrange("g (p j) c -> (g p) j c", j=PACK)
+
+        def load_packed(name, src, n0, n1):
+            raw = sb.tile([P, PACK, n1 - n0], F32, name=name)
+            nc.sync.dma_start(out=raw[:], in_=packed_view(src)[:, :, n0:n1])
+            return raw
+
+        def to_mx(name, raw, width):
+            grouped = sb.tile([P, width, PACK], BF16, name=name + "_bf", align_bytes=64)
+            dst, src = interleave_views(grouped[:], raw[:])
+            nc.vector.tensor_copy(out=dst, in_=src)
+            codes = sb.tile([P, width], U32, name=name + "_codes", align_bytes=64)
+            scales = sb.tile([P, width], U8, name=name + "_scales", align_bytes=64)
+            quantize(nc, codes[:], scales[:], grouped[:])
+            return codes, scales
+
+        w2_raw = load_packed("w2_raw", w2, 0, M)
+        x_raw = [load_packed("x_raw%d" % k, x, n0, n1) for k, (n0, n1) in enumerate(X_CHUNKS)]
+        w1_raw = load_packed("w1_raw", w1, 0, M)
+        fl_sb = sb.tile([P, G, 8], F32, name="fl_sb")
+        hs_sb = sb.tile([P, G, 8], F32, name="hs_sb")
+        with nc.allow_non_contiguous_dma(reason="one value to a partition and group"):
+            nc.sync.dma_start(out=fl_sb[:, :, 0:1], in_=fl.rearrange("g m o -> m g o"))
+            nc.sync.dma_start(out=hs_sb[:, :, 0:1], in_=hs.rearrange("g m o -> m g o"))
+        wo_raw = load_packed("wo_raw", wo2, 0, O)
+        res_sb = sb.tile([P, G, N], F32, name="res_sb")
+        nc.sync.dma_start(out=res_sb[:], in_=res.rearrange("g o n -> o g n"))
+
+        s2 = sb.tile([P, G, N], F32, name="s2")
+        e2 = sb.tile([P, G, N], F32, name="e2")
+        c1 = sb.tile([P, G, N], F32, name="c1")
+        s1 = sb.tile([P, G, N], F32, name="s1")
+        lg = sb.tile([P, G, N], F32, name="lg")
+        arg = sb.tile([P, G, N], F32, name="arg")
+        share = sb.tile([P, G, N], F32, name="share")
+
+        def square(k):
+            n0, n1 = X_CHUNKS[k]
+            for g in range(G):
+                nc.scalar.activation(out=s2[:, g, n0:n1], in_=bank_b[g][:, n0:n1], func=ACT.Square)
+
+        def bell(k, g0, g1):
+            n0, n1 = X_CHUNKS[k]
+            nc.scalar.activation(
+                out=e2[:, g0:g1, n0:n1], in_=s2[:, g0:g1, n0:n1], func=ACT.Exp, scale=-1.0
+            )
+
+        w2_mx = to_mx("w2", w2_raw, M)
+        x_mx = []
+        for k, (n0, n1) in enumerate(X_CHUNKS):
+            x_mx.append(to_mx("x%d" % k, x_raw[k], n1 - n0))
+            grouped_product(nc, bank_b, *w2_mx, *x_mx[k], n0, n1, n0)
+            if k == 2:
+                bell(0, 0, G)
+                bell(1, 0, G)
+            square(k)
+        bell(2, 0, 2)
+        bell(2, 2, G)
+
+        w1_mx = to_mx("w1", w1_raw, M)
+        for k, (n0, n1) in enumerate(X_CHUNKS):
+            grouped_product(nc, bank_a, *w1_mx, *x_mx[k], n0, n1, n0)
+        for g in range(G):
+            nc.vector.tensor_copy(out=c1[:, g, :], in_=bank_a[g][:])
+        for g in range(G):
+            nc.vector.tensor_tensor(out=s1[:, g, :], in0=c1[:, g, :], in1=c1[:, g, :], op=ALU.mult)
+        wo_mx = to_mx("wo", wo_raw, O)
+
+        for g in range(G):
+            nc.scalar.activation(
+                out=lg[:, g, :], in_=e2[:, g, :], func=ACT.Ln, bias=fl_sb[:, g, 0:1]
+            )
+            nc.vector.tensor_tensor(out=arg[:, g, :], in0=lg[:, g, :], in1=s1[:, g, :], op=ALU.add)
+
+        moved = []
+        for k, (n0, n1) in enumerate(H_CHUNKS):
+            nc.scalar.activation(
+                out=share[:, :, n0:n1], in_=arg[:, :, n0:n1], func=ACT.Sigmoid, scale=-1.0
+            )
+            hh = sb.tile([P, G, n1 - n0], BF16, name="hh%d" % k)
+            hh_moved = sb.tile([P, PACK, n1 - n0], BF16, name="hh_moved%d" % k)
+            moved.append(hh_moved)
+            for g in range(G):
+                nc.vector.scalar_tensor_tensor(
+                    out=hh[:, g, :],
+                    in0=bank_b[g][:, n0:n1],
+                    scalar=hs_sb[:, g, 0:1],
+                    in1=share[:, g, n0:n1],
+                    op0=ALU.mult,
+                    op1=ALU.mult,
+                )
+                nc.sync.dma_start(out=hh_moved[ROWS * g : ROWS * (g + 1), :, :], in_=hh[:, g, :])
+
+        def second_layer(k):
+            n0, n1 = H_CHUNKS[k]
+            width = n1 - n0
+            grouped = sb.tile([P, width, PACK], BF16, name="hh_bf%d" % k, align_bytes=64)
+            dst, src = interleave_views(grouped[:], moved[k][:])
+            if k == len(H_CHUNKS) - 1:
+                cut = width // 8
+                nc.scalar.copy(out=dst[:, 0 : cut - 4], in_=src[:, 0 : cut - 4])
+                nc.vector.tensor_copy(out=dst[:, cut - 4 :], in_=src[:, cut - 4 :])
+            else:
+                nc.scalar.copy(out=dst, in_=src)
+            codes = sb.tile([P, width], U32, name="hh_codes%d" % k, align_bytes=64)
+            scales = sb.tile([P, width], U8, name="hh_scales%d" % k, align_bytes=64)
+            quantize(nc, codes[:], scales[:], grouped[:])
+            grouped_product(nc, (bank_a, bank_b)[k % 2], *wo_mx, codes, scales, n0, n1, n0)
+
+        def finish(k):
+            n0, n1 = H_CHUNKS[k]
+            y = sb.tile([P, G, n1 - n0], F32, name="y%d" % k)
+            for g in range(G):
+                nc.vector.tensor_tensor(
+                    out=y[:, g, :], in0=(bank_a, bank_b)[k % 2][g][:, n0:n1], in1=res_sb[:, g, n0:n1], op=ALU.add
+                )
+                if g % 2 == 1:
+                    nc.sync.dma_start(
+                        out=out.rearrange("g o n -> o g n")[:, g - 1 : g + 1, n0:n1],
+                        in_=y[:, g - 1 : g + 1, :],
+                    )
+
+        second_layer(0)
+        for k in range(1, len(H_CHUNKS)):
+            second_layer(k)
+            finish(k - 1)
+        finish(len(H_CHUNKS) - 1)

@@ -18,7 +18,7 @@ PACK = 4
 ROWS = 32
 NMM = 128
 X_CHUNKS = ((0, 128), (128, 256), (256, 512))
-H_CHUNKS = ((0, 128), (128, 256), (256, 384), (384, 512))
+HALF = 256
 
 
 def interleave_views(grouped, raw):
@@ -34,17 +34,18 @@ def quantize(nc, codes, scales, grouped):
     )
 
 
-def grouped_product(nc, banks, w_codes, w_scales, codes, scales, n0, n1, off):
-    for c0 in range(n0, n1, NMM):
-        for g in range(G):
-            rows = slice(ROWS * g, ROWS * (g + 1))
-            cols = slice(c0 - off, c0 - off + NMM)
+def grouped_product(nc, banks, place, w_mx, in_mx, c0, c1):
+    w_codes, w_scales = w_mx
+    codes, scales = in_mx
+    for g in range(G):
+        rows = slice(ROWS * g, ROWS * (g + 1))
+        for c in range(c0, c1, NMM):
             nc.tensor.matmul_mx(
-                out=banks[g][:, c0 : c0 + NMM],
+                out=banks[g][:, place + c - c0 : place + c - c0 + NMM],
                 lhsT=w_codes[rows, :].bitcast(FP8X4),
                 lhsT_scale=w_scales[rows, :],
-                rhs=codes[rows, cols].bitcast(FP8X4),
-                rhs_scale=scales[rows, cols],
+                rhs=codes[rows, c : c + NMM].bitcast(FP8X4),
+                rhs_scale=scales[rows, c : c + NMM],
                 start=True,
                 stop=True,
             )
@@ -60,22 +61,26 @@ def tile_rows_fgaussshare_kernel(tc, x, w1, w2, fl, hs, wo2, res, out):
         bank_a = [ps.tile([P, N], F32, name="bank_a%d" % g) for g in range(G)]
         bank_b = [ps.tile([P, N], F32, name="bank_b%d" % g) for g in range(G)]
 
-        def packed_view(t):
-            return t.rearrange("g (p j) c -> (g p) j c", j=PACK)
-
         def load_packed(name, src, n0, n1):
             raw = sb.tile([P, PACK, n1 - n0], F32, name=name)
-            nc.sync.dma_start(out=raw[:], in_=packed_view(src)[:, :, n0:n1])
+            view = src.rearrange("g (p j) c -> (g p) j c", j=PACK)
+            nc.sync.dma_start(out=raw[:], in_=view[:, :, n0:n1])
             return raw
+
+        def quantized(name, grouped, width):
+            codes = sb.tile([P, width], U32, name=name + "_codes", align_bytes=64)
+            scales = sb.tile([P, width], U8, name=name + "_scales", align_bytes=64)
+            quantize(nc, codes[:], scales[:], grouped[:])
+            return codes, scales
 
         def to_mx(name, raw, width):
             grouped = sb.tile([P, width, PACK], BF16, name=name + "_bf", align_bytes=64)
             dst, src = interleave_views(grouped[:], raw[:])
             nc.vector.tensor_copy(out=dst, in_=src)
-            codes = sb.tile([P, width], U32, name=name + "_codes", align_bytes=64)
-            scales = sb.tile([P, width], U8, name=name + "_scales", align_bytes=64)
-            quantize(nc, codes[:], scales[:], grouped[:])
-            return codes, scales
+            return quantized(name, grouped, width)
+
+        def to_row_tile(dst, src, g):
+            nc.sync.dma_start(out=dst[ROWS * g : ROWS * (g + 1), :, :], in_=src[:, g, :])
 
         w2_raw = load_packed("w2_raw", w2, 0, M)
         x_raw = [load_packed("x_raw%d" % k, x, n0, n1) for k, (n0, n1) in enumerate(X_CHUNKS)]
@@ -83,24 +88,32 @@ def tile_rows_fgaussshare_kernel(tc, x, w1, w2, fl, hs, wo2, res, out):
         fl_sb = sb.tile([P, G, 8], F32, name="fl_sb")
         hs_sb = sb.tile([P, G, 8], F32, name="hs_sb")
         with nc.allow_non_contiguous_dma(reason="one value to a partition and group"):
-            nc.sync.dma_start(out=fl_sb[:, :, 0:1], in_=fl.rearrange("g m o -> m g o"))
             nc.sync.dma_start(out=hs_sb[:, :, 0:1], in_=hs.rearrange("g m o -> m g o"))
-        wo_raw = load_packed("wo_raw", wo2, 0, O)
+            nc.sync.dma_start(out=fl_sb[:, :, 0:1], in_=fl.rearrange("g m o -> m g o"))
         res_sb = sb.tile([P, G, N], F32, name="res_sb")
         nc.sync.dma_start(out=res_sb[:], in_=res.rearrange("g o n -> o g n"))
+        wo_raw = load_packed("wo_raw", wo2, 0, O)
 
         s2 = sb.tile([P, G, N], F32, name="s2")
         e2 = sb.tile([P, G, N], F32, name="e2")
-        c1 = sb.tile([P, G, N], F32, name="c1")
-        s1 = sb.tile([P, G, N], F32, name="s1")
         lg = sb.tile([P, G, N], F32, name="lg")
-        arg = sb.tile([P, G, N], F32, name="arg")
-        share = sb.tile([P, G, N], F32, name="share")
+        c1 = [sb.tile([P, G, HALF], F32, name="c1_%d" % h) for h in range(2)]
+        s1 = [sb.tile([P, G, HALF], F32, name="s1_%d" % h) for h in range(2)]
+        arg = [sb.tile([P, G, HALF], F32, name="arg_%d" % h) for h in range(2)]
+        c2 = sb.tile([P, G, HALF], F32, name="c2")
+        c2_moved = sb.tile([P, PACK, HALF], F32, name="c2_moved")
+        arg_moved = sb.tile([P, PACK, HALF], F32, name="arg_moved")
+        share_moved = sb.tile([P, PACK, HALF], F32, name="share_moved")
+        share = sb.tile([P, G, HALF], F32, name="share")
+        hh = sb.tile([P, G, HALF], BF16, name="hh")
+        hh_moved = sb.tile([P, PACK, HALF], BF16, name="hh_moved")
+        banks = (bank_a, bank_b)
 
         def square(k):
             n0, n1 = X_CHUNKS[k]
             for g in range(G):
-                nc.scalar.activation(out=s2[:, g, n0:n1], in_=bank_b[g][:, n0:n1], func=ACT.Square)
+                src = banks[n0 // HALF][g][:, n0 % HALF : n0 % HALF + n1 - n0]
+                nc.scalar.activation(out=s2[:, g, n0:n1], in_=src, func=ACT.Square)
 
         def bell(k, g0, g1):
             n0, n1 = X_CHUNKS[k]
@@ -112,7 +125,7 @@ def tile_rows_fgaussshare_kernel(tc, x, w1, w2, fl, hs, wo2, res, out):
         x_mx = []
         for k, (n0, n1) in enumerate(X_CHUNKS):
             x_mx.append(to_mx("x%d" % k, x_raw[k], n1 - n0))
-            grouped_product(nc, bank_b, *w2_mx, *x_mx[k], n0, n1, n0)
+            grouped_product(nc, banks[n0 // HALF], n0 % HALF, w2_mx, x_mx[k], 0, n1 - n0)
             if k == 2:
                 bell(0, 0, G)
                 bell(1, 0, G)
@@ -121,70 +134,113 @@ def tile_rows_fgaussshare_kernel(tc, x, w1, w2, fl, hs, wo2, res, out):
         bell(2, 2, G)
 
         w1_mx = to_mx("w1", w1_raw, M)
+        for g in range(G):
+            nc.vector.tensor_scalar(
+                out=c2[:, g, :],
+                in0=bank_a[g][:, 0:HALF],
+                scalar1=hs_sb[:, g, 0:1],
+                scalar2=None,
+                op0=ALU.mult,
+            )
+            to_row_tile(c2_moved, c2, g)
         for k, (n0, n1) in enumerate(X_CHUNKS):
-            grouped_product(nc, bank_a, *w1_mx, *x_mx[k], n0, n1, n0)
-        for g in range(G):
-            nc.vector.tensor_copy(out=c1[:, g, :], in_=bank_a[g][:])
-        for g in range(G):
-            nc.vector.tensor_tensor(out=s1[:, g, :], in0=c1[:, g, :], in1=c1[:, g, :], op=ALU.mult)
-        wo_mx = to_mx("wo", wo_raw, O)
+            grouped_product(nc, banks[n0 // HALF], HALF + n0 % HALF, w1_mx, x_mx[k], 0, n1 - n0)
+        for h in range(2):
+            for g in range(G):
+                nc.vector.tensor_copy(out=c1[h][:, g, :], in_=banks[h][g][:, HALF:N])
+            for g0 in (0, 2):
+                nc.vector.tensor_tensor(
+                    out=s1[h][:, g0 : g0 + 2, :],
+                    in0=c1[h][:, g0 : g0 + 2, :],
+                    in1=c1[h][:, g0 : g0 + 2, :],
+                    op=ALU.mult,
+                )
+
+        wo_bf = sb.tile([P, O, PACK], BF16, name="wo_bf", align_bytes=64)
+        dst, src = interleave_views(wo_bf[:], wo_raw[:])
+        nc.gpsimd.tensor_scalar(
+            out=dst, in0=src, scalar1=1.0, scalar2=0.0, op0=ALU.mult, op1=ALU.add
+        )
 
         for g in range(G):
             nc.scalar.activation(
                 out=lg[:, g, :], in_=e2[:, g, :], func=ACT.Ln, bias=fl_sb[:, g, 0:1]
             )
-            nc.vector.tensor_tensor(out=arg[:, g, :], in0=lg[:, g, :], in1=s1[:, g, :], op=ALU.add)
-
-        moved = []
-        for k, (n0, n1) in enumerate(H_CHUNKS):
-            nc.scalar.activation(
-                out=share[:, :, n0:n1], in_=arg[:, :, n0:n1], func=ACT.Sigmoid, scale=-1.0
+            nc.vector.tensor_tensor(
+                out=arg[0][:, g, :], in0=lg[:, g, 0:HALF], in1=s1[0][:, g, :], op=ALU.add
             )
-            hh = sb.tile([P, G, n1 - n0], BF16, name="hh%d" % k)
-            hh_moved = sb.tile([P, PACK, n1 - n0], BF16, name="hh_moved%d" % k)
-            moved.append(hh_moved)
-            for g in range(G):
-                nc.vector.scalar_tensor_tensor(
-                    out=hh[:, g, :],
-                    in0=bank_b[g][:, n0:n1],
-                    scalar=hs_sb[:, g, 0:1],
-                    in1=share[:, g, n0:n1],
-                    op0=ALU.mult,
-                    op1=ALU.mult,
-                )
-                nc.sync.dma_start(out=hh_moved[ROWS * g : ROWS * (g + 1), :, :], in_=hh[:, g, :])
+            to_row_tile(arg_moved, arg[0], g)
+        nc.vector.tensor_tensor(out=arg[1][:], in0=lg[:, :, HALF:N], in1=s1[1][:], op=ALU.add)
 
-        def second_layer(k):
-            n0, n1 = H_CHUNKS[k]
-            width = n1 - n0
-            grouped = sb.tile([P, width, PACK], BF16, name="hh_bf%d" % k, align_bytes=64)
-            dst, src = interleave_views(grouped[:], moved[k][:])
-            if k == len(H_CHUNKS) - 1:
-                cut = width // 8
-                nc.scalar.copy(out=dst[:, 0 : cut - 4], in_=src[:, 0 : cut - 4])
-                nc.vector.tensor_copy(out=dst[:, cut - 4 :], in_=src[:, cut - 4 :])
-            else:
-                nc.scalar.copy(out=dst, in_=src)
-            codes = sb.tile([P, width], U32, name="hh_codes%d" % k, align_bytes=64)
-            scales = sb.tile([P, width], U8, name="hh_scales%d" % k, align_bytes=64)
-            quantize(nc, codes[:], scales[:], grouped[:])
-            grouped_product(nc, (bank_a, bank_b)[k % 2], *wo_mx, codes, scales, n0, n1, n0)
+        for g in range(G):
+            nc.scalar.activation(
+                out=share[:, g, :], in_=arg[1][:, g, :], func=ACT.Sigmoid, scale=-1.0
+            )
+            nc.vector.scalar_tensor_tensor(
+                out=hh[:, g, :],
+                in0=bank_b[g][:, 0:HALF],
+                scalar=hs_sb[:, g, 0:1],
+                in1=share[:, g, :],
+                op0=ALU.mult,
+                op1=ALU.mult,
+            )
+            to_row_tile(hh_moved, hh, g)
 
-        def finish(k):
-            n0, n1 = H_CHUNKS[k]
-            y = sb.tile([P, G, n1 - n0], F32, name="y%d" % k)
-            for g in range(G):
+        grouped = [
+            sb.tile([P, NMM, PACK], BF16, name="hh_bf%d" % k, align_bytes=64) for k in range(4)
+        ]
+
+        def early_hh(k):
+            cols = slice(NMM * k, NMM * (k + 1))
+            nc.scalar.activation(
+                out=share_moved[:, :, cols], in_=arg_moved[:, :, cols], func=ACT.Sigmoid, scale=-1.0
+            )
+            nc.vector.tensor_tensor(
+                out=grouped[k][:].rearrange("p (c i) j -> p c j i", i=2),
+                in0=c2_moved[:, :, cols].rearrange("p j (c i) -> p c j i", i=2),
+                in1=share_moved[:, :, cols].rearrange("p j (c i) -> p c j i", i=2),
+                op=ALU.mult,
+            )
+
+        def late_interleave(k):
+            dst, src = interleave_views(
+                grouped[k][:], hh_moved[:, :, NMM * k - HALF : NMM * (k + 1) - HALF]
+            )
+            nc.scalar.copy(out=dst, in_=src)
+
+        def second_product(k):
+            hh_mx = quantized("hh%d" % k, grouped[k], NMM)
+            grouped_product(nc, banks[k % 2], HALF, wo_mx, hh_mx, 0, NMM)
+
+        y = [sb.tile([P, G, NMM], F32, name="y%d" % k) for k in range(4)]
+        out_view = out.rearrange("g o n -> o g n")
+
+        def finish(k, g0, g1, store_from):
+            cols = slice(NMM * k, NMM * (k + 1))
+            for g in range(g0, g1):
                 nc.vector.tensor_tensor(
-                    out=y[:, g, :], in0=(bank_a, bank_b)[k % 2][g][:, n0:n1], in1=res_sb[:, g, n0:n1], op=ALU.add
+                    out=y[k][:, g, :],
+                    in0=banks[k % 2][g][:, HALF : HALF + NMM],
+                    in1=res_sb[:, g, cols],
+                    op=ALU.add,
                 )
-                if g % 2 == 1:
-                    nc.sync.dma_start(
-                        out=out.rearrange("g o n -> o g n")[:, g - 1 : g + 1, n0:n1],
-                        in_=y[:, g - 1 : g + 1, :],
-                    )
+            if store_from is not None:
+                nc.sync.dma_start(
+                    out=out_view[:, store_from:g1, cols], in_=y[k][:, store_from:g1, :]
+                )
 
-        second_layer(0)
-        for k in range(1, len(H_CHUNKS)):
-            second_layer(k)
-            finish(k - 1)
-        finish(len(H_CHUNKS) - 1)
+        early_hh(0)
+        wo_mx = quantized("wo", wo_bf, O)
+        second_product(0)
+        early_hh(1)
+        finish(0, 0, 2, None)
+        second_product(1)
+        finish(0, 2, G, 0)
+        late_interleave(2)
+        second_product(2)
+        finish(1, 0, G, 0)
+        late_interleave(3)
+        second_product(3)
+        finish(2, 0, G, 0)
+        finish(3, 0, 2, 0)
+        finish(3, 2, G, 2)

@@ -34,10 +34,10 @@ def quantize(nc, codes, scales, grouped):
     )
 
 
-def grouped_product(nc, banks, place, w_mx, in_mx, c0, c1):
+def grouped_product(nc, banks, place, w_mx, in_mx, c0, c1, groups=range(G)):
     w_codes, w_scales = w_mx
     codes, scales = in_mx
-    for g in range(G):
+    for g in groups:
         rows = slice(ROWS * g, ROWS * (g + 1))
         for c in range(c0, c1, NMM):
             nc.tensor.matmul_mx(
@@ -60,6 +60,9 @@ def tile_rows_fgaussshare_kernel(tc, x, w1, w2, fl, hs, wo2, res, out):
 
         bank_a = [ps.tile([P, N], F32, name="bank_a%d" % g) for g in range(G)]
         bank_b = [ps.tile([P, N], F32, name="bank_b%d" % g) for g in range(G)]
+        rows_sb = sb.tile([P, P], F32, name="rows_sb", align_bytes=64)
+        cols_sb = sb.tile([P, P], F32, name="cols_sb", align_bytes=64)
+        nc.vector.memset(rows_sb[:], 0.0)
 
         def load_packed(name, src, n0, n1):
             raw = sb.tile([P, PACK, n1 - n0], F32, name=name)
@@ -84,15 +87,17 @@ def tile_rows_fgaussshare_kernel(tc, x, w1, w2, fl, hs, wo2, res, out):
 
         w2_raw = load_packed("w2_raw", w2, 0, M)
         x_raw = [load_packed("x_raw%d" % k, x, n0, n1) for k, (n0, n1) in enumerate(X_CHUNKS)]
+        for r, vec in enumerate((fl, hs)):
+            nc.scalar.dma_start(
+                out=rows_sb[r:P:ROWS, :].rearrange("q (g i) -> q g i", g=G),
+                in_=vec.rearrange("g (q i) o -> q g (i o)", i=ROWS),
+            )
         w1_raw = load_packed("w1_raw", w1, 0, M)
-        fl_sb = sb.tile([P, G, 8], F32, name="fl_sb")
-        hs_sb = sb.tile([P, G, 8], F32, name="hs_sb")
-        with nc.allow_non_contiguous_dma(reason="one value to a partition and group"):
-            nc.sync.dma_start(out=hs_sb[:, :, 0:1], in_=hs.rearrange("g m o -> m g o"))
-            nc.sync.dma_start(out=fl_sb[:, :, 0:1], in_=fl.rearrange("g m o -> m g o"))
+        wo_raw = load_packed("wo_raw", wo2, 0, O)
         res_sb = sb.tile([P, G, N], F32, name="res_sb")
         nc.sync.dma_start(out=res_sb[:], in_=res.rearrange("g o n -> o g n"))
-        wo_raw = load_packed("wo_raw", wo2, 0, O)
+        fl_col = [cols_sb[:, ROWS * g : ROWS * g + 1] for g in range(G)]
+        hs_col = [cols_sb[:, ROWS * g + 1 : ROWS * g + 2] for g in range(G)]
 
         s2 = sb.tile([P, G, N], F32, name="s2")
         e2 = sb.tile([P, G, N], F32, name="e2")
@@ -103,7 +108,7 @@ def tile_rows_fgaussshare_kernel(tc, x, w1, w2, fl, hs, wo2, res, out):
         c2 = sb.tile([P, G, HALF], F32, name="c2")
         c2_moved = sb.tile([P, PACK, HALF], F32, name="c2_moved")
         arg_moved = sb.tile([P, PACK, HALF], F32, name="arg_moved")
-        share_moved = sb.tile([P, PACK, HALF], F32, name="share_moved")
+        share_moved = sb.tile([P, HALF, PACK], F32, name="share_moved")
         share = sb.tile([P, G, HALF], F32, name="share")
         hh = sb.tile([P, G, HALF], BF16, name="hh")
         hh_moved = sb.tile([P, PACK, HALF], BF16, name="hh_moved")
@@ -124,6 +129,8 @@ def tile_rows_fgaussshare_kernel(tc, x, w1, w2, fl, hs, wo2, res, out):
         w2_mx = to_mx("w2", w2_raw, M)
         x_mx = []
         for k, (n0, n1) in enumerate(X_CHUNKS):
+            if k == 2:
+                nc.vector.transpose(out=cols_sb[:], in_=rows_sb[:])
             x_mx.append(to_mx("x%d" % k, x_raw[k], n1 - n0))
             grouped_product(nc, banks[n0 // HALF], n0 % HALF, w2_mx, x_mx[k], 0, n1 - n0)
             if k == 2:
@@ -138,13 +145,15 @@ def tile_rows_fgaussshare_kernel(tc, x, w1, w2, fl, hs, wo2, res, out):
             nc.vector.tensor_scalar(
                 out=c2[:, g, :],
                 in0=bank_a[g][:, 0:HALF],
-                scalar1=hs_sb[:, g, 0:1],
+                scalar1=hs_col[g],
                 scalar2=None,
                 op0=ALU.mult,
             )
             to_row_tile(c2_moved, c2, g)
-        for k, (n0, n1) in enumerate(X_CHUNKS):
-            grouped_product(nc, banks[n0 // HALF], HALF + n0 % HALF, w1_mx, x_mx[k], 0, n1 - n0)
+            for k in (0, 1):
+                n0, n1 = X_CHUNKS[k]
+                grouped_product(nc, bank_a, HALF + n0, w1_mx, x_mx[k], 0, n1 - n0, (g,))
+        grouped_product(nc, bank_b, HALF, w1_mx, x_mx[2], 0, HALF)
         for h in range(2):
             for g in range(G):
                 nc.vector.tensor_copy(out=c1[h][:, g, :], in_=banks[h][g][:, HALF:N])
@@ -156,21 +165,16 @@ def tile_rows_fgaussshare_kernel(tc, x, w1, w2, fl, hs, wo2, res, out):
                     op=ALU.mult,
                 )
 
-        wo_bf = sb.tile([P, O, PACK], BF16, name="wo_bf", align_bytes=64)
-        dst, src = interleave_views(wo_bf[:], wo_raw[:])
-        nc.gpsimd.tensor_scalar(
-            out=dst, in0=src, scalar1=1.0, scalar2=0.0, op0=ALU.mult, op1=ALU.add
-        )
-
         for g in range(G):
             nc.scalar.activation(
-                out=lg[:, g, :], in_=e2[:, g, :], func=ACT.Ln, bias=fl_sb[:, g, 0:1]
+                out=lg[:, g, :], in_=e2[:, g, :], func=ACT.Ln, bias=fl_col[g]
             )
             nc.vector.tensor_tensor(
                 out=arg[0][:, g, :], in0=lg[:, g, 0:HALF], in1=s1[0][:, g, :], op=ALU.add
             )
             to_row_tile(arg_moved, arg[0], g)
         nc.vector.tensor_tensor(out=arg[1][:], in0=lg[:, :, HALF:N], in1=s1[1][:], op=ALU.add)
+        wo_mx = to_mx("wo", wo_raw, O)
 
         for g in range(G):
             nc.scalar.activation(
@@ -179,7 +183,7 @@ def tile_rows_fgaussshare_kernel(tc, x, w1, w2, fl, hs, wo2, res, out):
             nc.vector.scalar_tensor_tensor(
                 out=hh[:, g, :],
                 in0=bank_b[g][:, 0:HALF],
-                scalar=hs_sb[:, g, 0:1],
+                scalar=hs_col[g],
                 in1=share[:, g, :],
                 op0=ALU.mult,
                 op1=ALU.mult,
@@ -193,12 +197,15 @@ def tile_rows_fgaussshare_kernel(tc, x, w1, w2, fl, hs, wo2, res, out):
         def early_hh(k):
             cols = slice(NMM * k, NMM * (k + 1))
             nc.scalar.activation(
-                out=share_moved[:, :, cols], in_=arg_moved[:, :, cols], func=ACT.Sigmoid, scale=-1.0
+                out=share_moved[:, cols, :],
+                in_=arg_moved[:, :, cols].rearrange("p j n -> p n j"),
+                func=ACT.Sigmoid,
+                scale=-1.0,
             )
             nc.vector.tensor_tensor(
-                out=grouped[k][:].rearrange("p (c i) j -> p c j i", i=2),
-                in0=c2_moved[:, :, cols].rearrange("p j (c i) -> p c j i", i=2),
-                in1=share_moved[:, :, cols].rearrange("p j (c i) -> p c j i", i=2),
+                out=grouped[k][:],
+                in0=c2_moved[:, :, cols].rearrange("p j n -> p n j"),
+                in1=share_moved[:, cols, :],
                 op=ALU.mult,
             )
 
@@ -230,12 +237,10 @@ def tile_rows_fgaussshare_kernel(tc, x, w1, w2, fl, hs, wo2, res, out):
                 )
 
         early_hh(0)
-        wo_mx = quantized("wo", wo_bf, O)
-        second_product(0)
         early_hh(1)
-        finish(0, 0, 2, None)
+        second_product(0)
         second_product(1)
-        finish(0, 2, G, 0)
+        finish(0, 0, G, 0)
         late_interleave(2)
         second_product(2)
         finish(1, 0, G, 0)

from contextlib import ExitStack

import concourse.mybir as mybir

G, D, M, O, N = 4, 128, 128, 128, 512
FLOPS = 2 * G * N * (2 * D * M + M * O)

F32 = mybir.dt.float32
BF16 = mybir.dt.bfloat16
U32 = mybir.dt.uint32
U8 = mybir.dt.uint8
FP8X4 = mybir.dt.float8_e4m3fn_x4
ACT = mybir.ActivationFunctionType
ALU = mybir.AluOpType

P = 128
PACK = 4
ROWS = 32
NMM = 128
X_CHUNKS = ((0, 128), (128, 256), (256, 512))
HALF = 256


def interleave_views(grouped, raw):
    return (
        grouped.rearrange("p (c i) j -> p c j i", i=4),
        raw.rearrange("p j (c i) -> p c j i", i=4),
    )


def quantize(nc, codes, scales, grouped):
    nc.vector.quantize_mx(
        out=codes.bitcast(FP8X4), scales=scales, in_=grouped.rearrange("p w j -> p (w j)")
    )


def grouped_product(nc, banks, place, w_mx, in_mx, c0, c1, groups=range(G)):
    w_codes, w_scales = w_mx
    codes, scales = in_mx
    for g in groups:
        rows = slice(ROWS * g, ROWS * (g + 1))
        for c in range(c0, c1, NMM):
            nc.tensor.matmul_mx(
                out=banks[g][:, place + c - c0 : place + c - c0 + NMM],
                lhsT=w_codes[rows, :].bitcast(FP8X4),
                lhsT_scale=w_scales[rows, :],
                rhs=codes[rows, c : c + NMM].bitcast(FP8X4),
                rhs_scale=scales[rows, c : c + NMM],
                start=True,
                stop=True,
            )


def tile_rows_fgaussshare_kernel(tc, x, w1, w2, fl, hs, wo2, res, out):
    nc = tc.nc
    with ExitStack() as ctx:
        sb = ctx.enter_context(tc.tile_pool(name="sb", bufs=1))
        ps = ctx.enter_context(tc.psum_pool(name="ps", bufs=1))
        ctx.enter_context(tc.manual_schedule())

        bank_a = [ps.tile([P, N], F32, name="bank_a%d" % g) for g in range(G)]
        bank_b = [ps.tile([P, N], F32, name="bank_b%d" % g) for g in range(G)]
        rows_sb = sb.tile([P, P], F32, name="rows_sb", align_bytes=64)
        cols_sb = sb.tile([P, P], F32, name="cols_sb", align_bytes=64)
        nc.vector.memset(rows_sb[:], 0.0)

        def load_packed(name, src, n0, n1):
            raw = sb.tile([P, PACK, n1 - n0], F32, name=name)
            view = src.rearrange("g (p j) c -> (g p) j c", j=PACK)
            nc.sync.dma_start(out=raw[:], in_=view[:, :, n0:n1])
            return raw

        def quantized(name, grouped, width):
            codes = sb.tile([P, width], U32, name=name + "_codes", align_bytes=64)
            scales = sb.tile([P, width], U8, name=name + "_scales", align_bytes=64)
            quantize(nc, codes[:], scales[:], grouped[:])
            return codes, scales

        def to_mx(name, raw, width):
            grouped = sb.tile([P, width, PACK], BF16, name=name + "_bf", align_bytes=64)
            dst, src = interleave_views(grouped[:], raw[:])
            nc.vector.tensor_copy(out=dst, in_=src)
            return quantized(name, grouped, width)

        def to_row_tile(dst, src, g):
            nc.sync.dma_start(out=dst[ROWS * g : ROWS * (g + 1), :, :], in_=src[:, g, :])

        w2_raw = load_packed("w2_raw", w2, 0, M)
        x_raw = [load_packed("x_raw%d" % k, x, n0, n1) for k, (n0, n1) in enumerate(X_CHUNKS)]
        for r, vec in enumerate((fl, hs)):
            nc.scalar.dma_start(
                out=rows_sb[r:P:ROWS, :].rearrange("q (g i) -> q g i", g=G),
                in_=vec.rearrange("g (q i) o -> q g (i o)", i=ROWS),
            )
        w1_raw = load_packed("w1_raw", w1, 0, M)
        wo_raw = load_packed("wo_raw", wo2, 0, O)
        res_sb = sb.tile([P, G, N], F32, name="res_sb")
        nc.sync.dma_start(out=res_sb[:], in_=res.rearrange("g o n -> o g n"))
        fl_col = [cols_sb[:, ROWS * g : ROWS * g + 1] for g in range(G)]
        hs_col = [cols_sb[:, ROWS * g + 1 : ROWS * g + 2] for g in range(G)]

        s2 = sb.tile([P, G, N], F32, name="s2")
        e2 = sb.tile([P, G, N], F32, name="e2")
        lg = sb.tile([P, G, N], F32, name="lg")
        c1 = [sb.tile([P, G, HALF], F32, name="c1_%d" % h) for h in range(2)]
        s1 = [sb.tile([P, G, HALF], F32, name="s1_%d" % h) for h in range(2)]
        arg = [sb.tile([P, G, HALF], F32, name="arg_%d" % h) for h in range(2)]
        c2 = sb.tile([P, G, HALF], F32, name="c2")
        c2_moved = sb.tile([P, PACK, HALF], F32, name="c2_moved")
        arg_moved = sb.tile([P, PACK, HALF], F32, name="arg_moved")
        share_moved = sb.tile([P, HALF, PACK], F32, name="share_moved")
        share = sb.tile([P, G, HALF], F32, name="share")
        hh = sb.tile([P, G, HALF], BF16, name="hh")
        hh_moved = sb.tile([P, PACK, HALF], BF16, name="hh_moved")
        banks = (bank_a, bank_b)

        def square(k):
            n0, n1 = X_CHUNKS[k]
            for g in range(G):
                src = banks[n0 // HALF][g][:, n0 % HALF : n0 % HALF + n1 - n0]
                nc.scalar.activation(out=s2[:, g, n0:n1], in_=src, func=ACT.Square)

        def bell(k, g0, g1):
            n0, n1 = X_CHUNKS[k]
            nc.scalar.activation(
                out=e2[:, g0:g1, n0:n1], in_=s2[:, g0:g1, n0:n1], func=ACT.Exp, scale=-1.0
            )

        w2_mx = to_mx("w2", w2_raw, M)
        x_mx = []
        for k, (n0, n1) in enumerate(X_CHUNKS):
            if k == 2:
                nc.vector.transpose(out=cols_sb[:], in_=rows_sb[:])
            x_mx.append(to_mx("x%d" % k, x_raw[k], n1 - n0))
            grouped_product(nc, banks[n0 // HALF], n0 % HALF, w2_mx, x_mx[k], 0, n1 - n0)
            if k == 2:
                bell(0, 0, G)
                bell(1, 0, G)
            square(k)
        bell(2, 0, 2)
        bell(2, 2, G)

        w1_mx = to_mx("w1", w1_raw, M)
        for g in range(G):
            nc.vector.tensor_scalar(
                out=c2[:, g, :],
                in0=bank_a[g][:, 0:HALF],
                scalar1=hs_col[g],
                scalar2=None,
                op0=ALU.mult,
            )
            to_row_tile(c2_moved, c2, g)
            for k in (0, 1):
                n0, n1 = X_CHUNKS[k]
                grouped_product(nc, bank_a, HALF + n0, w1_mx, x_mx[k], 0, n1 - n0, (g,))
        grouped_product(nc, bank_b, HALF, w1_mx, x_mx[2], 0, HALF)
        for h in range(2):
            for g in range(G):
                nc.vector.tensor_copy(out=c1[h][:, g, :], in_=banks[h][g][:, HALF:N])
            for g0 in (0, 2):
                nc.vector.tensor_tensor(
                    out=s1[h][:, g0 : g0 + 2, :],
                    in0=c1[h][:, g0 : g0 + 2, :],
                    in1=c1[h][:, g0 : g0 + 2, :],
                    op=ALU.mult,
                )

        for g in range(G):
            nc.scalar.activation(
                out=lg[:, g, :], in_=e2[:, g, :], func=ACT.Ln, bias=fl_col[g]
            )
            nc.vector.tensor_tensor(
                out=arg[0][:, g, :], in0=lg[:, g, 0:HALF], in1=s1[0][:, g, :], op=ALU.add
            )
            to_row_tile(arg_moved, arg[0], g)
        nc.vector.tensor_tensor(out=arg[1][:], in0=lg[:, :, HALF:N], in1=s1[1][:], op=ALU.add)
        wo_mx = to_mx("wo", wo_raw, O)

        for g in range(G):
            nc.scalar.activation(
                out=share[:, g, :], in_=arg[1][:, g, :], func=ACT.Sigmoid, scale=-1.0
            )
            nc.vector.scalar_tensor_tensor(
                out=hh[:, g, :],
                in0=bank_b[g][:, 0:HALF],
                scalar=hs_col[g],
                in1=share[:, g, :],
                op0=ALU.mult,
                op1=ALU.mult,
            )
            to_row_tile(hh_moved, hh, g)

        grouped = [
            sb.tile([P, NMM, PACK], BF16, name="hh_bf%d" % k, align_bytes=64) for k in range(4)
        ]

        def early_hh(k):
            cols = slice(NMM * k, NMM * (k + 1))
            nc.scalar.activation(
                out=share_moved[:, cols, :],
                in_=arg_moved[:, :, cols].rearrange("p j n -> p n j"),
                func=ACT.Sigmoid,
                scale=-1.0,
            )
            nc.vector.tensor_tensor(
                out=grouped[k][:],
                in0=c2_moved[:, :, cols].rearrange("p j n -> p n j"),
                in1=share_moved[:, cols, :],
                op=ALU.mult,
            )

        def late_interleave(k):
            dst, src = interleave_views(
                grouped[k][:], hh_moved[:, :, NMM * k - HALF : NMM * (k + 1) - HALF]
            )
            nc.scalar.copy(out=dst, in_=src)

        def second_product(k):
            hh_mx = quantized("hh%d" % k, grouped[k], NMM)
            grouped_product(nc, banks[k % 2], HALF, wo_mx, hh_mx, 0, NMM)

        y = [sb.tile([P, G, NMM], F32, name="y%d" % k) for k in range(4)]
        out_view = out.rearrange("g o n -> o g n")

        def finish(k, g0, g1, store_from):
            cols = slice(NMM * k, NMM * (k + 1))
            for g in range(g0, g1):
                nc.vector.tensor_tensor(
                    out=y[k][:, g, :],
                    in0=banks[k % 2][g][:, HALF : HALF + NMM],
                    in1=res_sb[:, g, cols],
                    op=ALU.add,
                )
            if store_from is not None:
                nc.sync.dma_start(
                    out=out_view[:, store_from:g1, cols], in_=y[k][:, store_from:g1, :]
                )

        early_hh(0)
        early_hh(1)
        second_product(0)
        second_product(1)
        finish(0, 0, G, 0)
        late_interleave(2)
        second_product(2)
        finish(1, 0, G, 0)
        late_interleave(3)
        second_product(3)
        finish(2, 0, G, 0)
        finish(3, 0, 2, 0)
        finish(3, 2, G, 2)
